import numpy as np
import ml_dtypes


def mxq(x, axis, fmt="e4m3"):
    dtype, down = {"e4m3": (ml_dtypes.float8_e4m3fn, 7), "e5m2": (ml_dtypes.float8_e5m2, 14)}[fmt]
    v = np.moveaxis(np.asarray(x, np.float32).astype(ml_dtypes.bfloat16).astype(np.float64), axis, -1)
    blocks = v.reshape(v.shape[:-1] + (-1, 32))
    amax = np.abs(blocks).max(-1, keepdims=True)
    byte = np.maximum(np.where(amax > 0, np.frexp(amax)[1] - 1 + 127, 0) - down, 1)
    scale = np.exp2(byte - 127.0)
    codes = (blocks / scale).astype(np.float32).astype(dtype).astype(np.float64)
    return np.moveaxis((codes * scale).reshape(v.shape), -1, axis)


WIDE = False


def mx_kscale(k):
    if not WIDE:
        return np.ones(k)
    levels = np.array([10, -10, 5, -5, 0])
    if k % 512:
        return np.exp2(np.random.permutation(np.resize(levels, k // 32))).repeat(32)
    a = np.empty((k // 512, 16))
    for p in range(k // 512):
        a[p, :8] = np.random.permutation(np.resize(levels, 8))
        for g in range(8):
            far = levels[np.abs(levels - a[p, g]) >= 10]
            a[p, g + 8] = far[np.random.randint(len(far))]
    return np.exp2(a.ravel()).repeat(32)


def f64(x):
    return np.asarray(x).astype(np.float64)


def striped(idx):
    return np.tile(idx.reshape(-1, 16).T, (8, 1)).astype(np.uint16)


def unstriped(offs):
    return offs[:16].T.reshape(-1).astype(np.int64)


E2M1 = np.array([0.0, 0.5, 1.0, 1.5, 2.0, 3.0, 4.0, 6.0, -0.0, -0.5, -1.0, -1.5, -2.0, -3.0, -4.0, -6.0])


def pack_weight(w, fmt):
    k, n = w.shape
    w = f64(np.asarray(w, np.float32).astype(ml_dtypes.bfloat16)).reshape(k // 32, 32, n)
    amax = np.abs(w).max(1)
    if fmt == "e4m3":
        byte = np.frexp(amax)[1] - 1 + 127 - 7
    else:
        mant, ex = np.frexp(amax / 6.0)
        byte = np.where(mant > 0.5, ex, ex - 1) + 127
    byte = np.clip(np.where(amax > 0, byte, 1), 1, 254)
    scaled = (w * np.exp2(127.0 - byte)[:, None, :]).reshape(k, n).astype(np.float32)
    by_word = np.ascontiguousarray(scaled.reshape(k // 512, 128, 4, n).transpose(0, 1, 3, 2))
    if fmt == "e4m3":
        words = by_word.astype(ml_dtypes.float8_e4m3fn).view(np.uint8)
    else:
        c = by_word.astype(ml_dtypes.float4_e2m1fn).view(np.uint8) & 0xF
        words = (c[..., 0::2] | (c[..., 1::2] << 4)).reshape(k // 512, 128, 2 * n)
    return np.ascontiguousarray(words), np.ascontiguousarray(byte.astype(np.uint8).reshape(k // 512, 16, n))


def unpack_weight(words, scales, fmt):
    g, _, n = scales.shape
    words = np.ascontiguousarray(words).reshape(g, 128, n, -1)
    if fmt == "e4m3":
        vals = words.view(ml_dtypes.float8_e4m3fn).astype(np.float64)
    else:
        nib = np.empty((g, 128, n, 4), np.uint8)
        nib[..., 0::2] = words & 0xF
        nib[..., 1::2] = words >> 4
        vals = E2M1[nib]
    vals = vals * np.repeat(np.exp2(scales.astype(np.float64) - 127.0), 8, axis=1)[..., None]
    return vals.transpose(0, 1, 3, 2).reshape(g * 512, n)


def gelu(v):
    return 0.5 * v * (1.0 + np.tanh(np.sqrt(2.0 / np.pi) * (v + 0.044715 * v**3)))


K, H, N, T, S, P = 1024, 1024, 768, 2048, 1024, 512

def setup_inputs():
    n = np.random.standard_normal
    s = mx_kscale(K)[:, None]
    u = mx_kscale(H)[:, None]
    tab_words, tab_scales = pack_weight(n((K, T)) * s, "e4m3")
    w1 = 0.8 * n((K, H)) / np.sqrt(K) / s
    w2_words, w2_scales = pack_weight(0.8 * n((K, H)) / np.sqrt(K) / s, "e2m1")
    gain = np.random.uniform(1.5, 5.0, H) * u[:, 0]
    w3 = 1.5 * n((H, N)) / np.sqrt(H) / u
    return {
        "tab_words": tab_words, "tab_scales": tab_scales,
        "offs": striped(np.random.permutation(T)[:S]),
        "pos1": striped(np.random.permutation(S)[:P]),
        "pos2": striped(np.random.permutation(S)[:P]),
        "w1": w1.astype(np.float32),
        "w2_words": w2_words, "w2_scales": w2_scales,
        "gain": gain.astype(np.float32),
        "w3": w3.astype(np.float32),
    }

def reference(tab_words, tab_scales, offs, pos1, pos2, w1, w2_words, w2_scales, gain, w3):
    v = unpack_weight(tab_words, tab_scales, "e4m3")[:, unstriped(offs)]
    h = mxq(f64(w1), 0, "e4m3").T @ v
    g = unpack_weight(w2_words, w2_scales, "e2m1").T @ v
    top = h.max(axis=1)
    a = np.exp(h[:, unstriped(pos1)] - top[:, None])
    lead = np.maximum(h, g)
    c = lead[:, unstriped(pos2)]
    d = a * c * f64(gain)[:, None]
    return np.abs(mxq(f64(w3), 0, "e4m3").T @ mxq(d, 0, "e4m3"))

@@ -1,0 +1,293 @@
+from contextlib import ExitStack
+
+import concourse.mybir as mybir
+
+K, H, N, T, S, M = 1024, 1024, 768, 2048, 1024, 512
+FLOPS = 2 * K * H * S * 2 + 2 * H * N * M
+
+F32 = mybir.dt.float32
+BF16 = mybir.dt.bfloat16
+I32 = mybir.dt.int32
+U32 = mybir.dt.uint32
+U16 = mybir.dt.uint16
+U8 = mybir.dt.uint8
+FP8X4 = mybir.dt.float8_e4m3fn_x4
+FP4X4 = mybir.dt.float4_e2m1fn_x4
+ALU = mybir.AluOpType
+ACT = mybir.ActivationFunctionType
+
+P = 128
+PACK = 4
+PASS = P * PACK
+BANK = 512
+KP = K // PASS
+HP = H // PASS
+HALF = M // 2
+
+
+def tile_list_trisomy_bin_deviation_kernel(
+    tc, tab_words, tab_scales, offs, pos1, pos2, w1, w2_words, w2_scales, gain, w3, out
+):
+    nc = tc.nc
+    with ExitStack() as ctx:
+        keep = ctx.enter_context(tc.tile_pool(name="keep", bufs=1))
+        two = ctx.enter_context(tc.tile_pool(name="two", bufs=2))
+        three = ctx.enter_context(tc.tile_pool(name="three", bufs=3))
+        psum = ctx.enter_context(tc.psum_pool(name="psum", bufs=8))
+
+        def held(shape, dtype, name):
+            return keep.tile(shape, dtype, name=name, align_bytes=64)
+
+        offs_t = keep.tile([P, S // 16], U16, name="offs_t")
+        pos1_t = keep.tile([P, M // 16], U16, name="pos1_t")
+        pos2_t = keep.tile([P, M // 16], U16, name="pos2_t")
+
+        tab_w = [held([P, T], I32, "tab_w%d" % a) for a in range(KP)]
+        tab_s = held([P, T], U8, "tab_s")
+        v_w = [held([P, S], U32, "v_w%d" % a) for a in range(KP)]
+        v_s = held([P, S], U8, "v_s")
+        v_s1 = held([P, S], U8, "v_s1")
+        w2s_raw = held([P, KP, H], U8, "w2s_raw")
+        w2s = held([P, KP, H], U8, "w2s")
+        w2w_raw = [held([P, KP, PASS // 2], I32, "w2w_raw%d" % b) for b in range(HP)]
+        w2w = [held([P, KP, 2 * PASS], U8, "w2w%d" % b) for b in range(HP)]
+        gain_t = [held([P, PACK], F32, "gain_t%d" % b) for b in range(HP)]
+        w1_codes = [[held([P, PASS], U32, "w1c%d%d" % (a, b)) for b in range(HP)] for a in range(KP)]
+        w1_scales = [[held([P, PASS], U8, "w1s%d%d" % (a, b)) for b in range(HP)] for a in range(KP)]
+        w3_codes = [held([P, N], U32, "w3c%d" % b) for b in range(HP)]
+        w3_scales = [held([P, N], U8, "w3s%d" % b) for b in range(HP)]
+        d_codes = [held([P, M], U32, "dc%d" % b) for b in range(HP)]
+        d_scales = [held([P, M], U8, "ds%d" % b) for b in range(HP)]
+
+        nc.vector.memset(tab_s[:].bitcast(I32), 0)
+        nc.gpsimd.memset(w2s_raw[:].rearrange("p a n -> p (a n)").bitcast(I32), 0)
+        nc.gpsimd.memset(v_s1[:].bitcast(I32), 0)
+
+        def load_tab_words(a):
+            nc.sync.dma_start(tab_w[a][:], tab_words[a].rearrange("p t i -> p (t i)").bitcast(I32))
+
+        def load_w1(a, b, c0, width, name):
+            raw = held([P, PACK, width], F32, name)
+            rows = w1[a * PASS : (a + 1) * PASS, b * PASS + c0 : b * PASS + c0 + width]
+            nc.sync.dma_start(raw[:], rows.rearrange("(p j) c -> p j c", j=PACK))
+            return raw
+
+        def load_w2_words(b):
+            src = w2_words.bitcast(I32)[:, :, b * (PASS // 2) : (b + 1) * (PASS // 2)]
+            nc.sync.dma_start(w2w_raw[b][:], src.rearrange("a p n -> p a n"))
+
+        def weave_w1(copy, grouped, raw, r0, c0, width):
+            w0, w1n = c0 // 16, (c0 + width) // 16
+            dst = grouped[:].rearrange("p (t w v j) -> p w t j v", t=PACK, v=4, j=PACK)[:, w0:w1n]
+            src = raw[:, :, r0 : r0 + width].rearrange("p j (w t v) -> p w t j v", t=PACK, v=4)
+            copy(dst, src)
+
+        def quantize(codes, scales, grouped, c0, c1, g0=0):
+            nc.vector.quantize_mx(
+                out=codes[:, c0:c1].bitcast(FP8X4),
+                scales=scales[:, c0:c1],
+                in_=grouped[:, PACK * (c0 - g0) : PACK * (c1 - g0)],
+            )
+
+        def deal_w2_words(b):
+            for a in range(KP):
+                dst = w2w[b][:, a, :].bitcast(U32).rearrange("p (t w u) -> p w t u", t=PACK, u=2)
+                src = w2w_raw[b][:, a, :].bitcast(U32).rearrange("p (w t u) -> p w t u", t=PACK, u=2)
+                nc.scalar.copy(dst, src)
+
+        nc.sync.dma_start(offs_t[:], offs)
+        load_tab_words(0)
+        ts32 = tab_scales.bitcast(I32)
+        for q in range(4):
+            nc.sync.dma_start(tab_s[:].bitcast(I32)[32 * q : 32 * q + 4 * KP, :], ts32[:, 4 * q : 4 * q + 4, :])
+        raw00 = load_w1(0, 0, 0, PASS, "w1raw00")
+        load_tab_words(1)
+        w2s32 = w2_scales.bitcast(I32)
+        for q in range(4):
+            nc.sync.dma_start(
+                w2s_raw[:].bitcast(I32)[32 * q : 32 * q + 4, :, :],
+                w2s32[:, 4 * q : 4 * q + 4, :].rearrange("a r n -> r a n"),
+            )
+        raw10 = [load_w1(1, 0, c0, PASS // 2, "w1raw10_%d" % c0) for c0 in (0, PASS // 2)]
+        load_w2_words(0)
+
+        nc.vector.tensor_copy(v_w[0][:], tab_w[0][:].bitcast(U32).indirect(offs_t[:]))
+        nc.vector.tensor_copy(v_s[:], tab_s[:].indirect(offs_t[:]))
+        nc.vector.tensor_copy(v_w[1][:], tab_w[1][:].bitcast(U32).indirect(offs_t[:]))
+        for q in range(4):
+            nc.sync.dma_start(
+                v_s1[:].bitcast(I32)[32 * q : 32 * q + 4, :], v_s[:].bitcast(I32)[32 * q + 4 : 32 * q + 8, :]
+            )
+        nc.sync.dma_start(pos1_t[:], pos1)
+        nc.sync.dma_start(pos2_t[:], pos2)
+        gain_v = gain.rearrange("(b w t v) -> b v w t", b=HP, t=PACK, v=4)
+
+        def load_gain(b):
+            with nc.allow_non_contiguous_dma(reason="one gain for each row of a slice"):
+                for v in range(4):
+                    nc.sync.dma_start(gain_t[b][v:P:4, :], gain_v[b, v])
+
+        load_gain(0)
+
+        g00 = two.tile([P, PACK * PASS], BF16, name="w1g", align_bytes=64)
+        for c0 in (0, PASS // 2):
+            weave_w1(nc.scalar.copy, g00, raw00, c0, c0, PASS // 2)
+        quantize(w1_codes[0][0], w1_scales[0][0], g00, 0, PASS)
+        g10 = two.tile([P, PACK * PASS], BF16, name="w1g", align_bytes=64)
+        weave_w1(nc.scalar.copy, g10, raw10[0], 0, 0, PASS // 2)
+        weave_w1(nc.vector.tensor_copy, g10, raw10[1], 0, PASS // 2, PASS // 2)
+        quantize(w1_codes[1][0], w1_scales[1][0], g10, 0, P)
+        quantize(w1_codes[1][0], w1_scales[1][0], g10, P, PASS)
+
+        dst = w2s[:].rearrange("p a n -> p (a n)").bitcast(U32).rearrange("p (c t w) -> p c w t", t=PACK, w=32)
+        src = w2s_raw[:].rearrange("p a n -> p (a n)").bitcast(U32).rearrange("p (c w t) -> p c w t", t=PACK, w=32)
+        nc.scalar.copy(dst, src)
+        deal_w2_words(0)
+
+        raw_b1 = [load_w1(a, 1, 0, PASS, "w1raw%d1" % a) for a in range(KP)]
+        load_w2_words(1)
+        load_gain(1)
+        w3_raw = []
+        for b in range(HP):
+            raw = held([P, PACK, N], F32, "w3raw%d" % b)
+            rows = w3[b * PASS : (b + 1) * PASS, :].rearrange("(w t v) n -> t w v n", t=PACK, v=4)
+            for t in range(PACK):
+                nc.sync.dma_start(raw[:, t, :], rows[t])
+            w3_raw.append(raw)
+
+        def prepare_w1_b1(a):
+            grouped = two.tile([P, PACK * PASS], BF16, name="w1g", align_bytes=64)
+            for c0 in (0, PASS // 2):
+                weave_w1(nc.scalar.copy, grouped, raw_b1[a], c0, c0, PASS // 2)
+            quantize(w1_codes[a][1], w1_scales[a][1], grouped, 0, PASS)
+
+        def weave(copy, grouped, planes, c0, c1, g0=0):
+            dst = grouped[:, PACK * (c0 - g0) : PACK * (c1 - g0)].rearrange("p (c i t) -> p c t i", i=4, t=PACK)
+            src = planes[:, :, c0:c1].rearrange("p t (c i) -> p c t i", i=4)
+            copy(dst, src)
+
+        def prepare_w3(b, part):
+            c0, c1 = part * (N // 2), (part + 1) * (N // 2)
+            grouped = two.tile([P, PACK * (N // 2)], BF16, name="w3g", align_bytes=64)
+            mid = (c0 + c1) // 2
+            weave(nc.scalar.copy, grouped, w3_raw[b], c0, mid, c0)
+            weave(nc.scalar.copy, grouped, w3_raw[b], mid, c1, c0)
+            quantize(w3_codes[b], w3_scales[b], grouped, c0, c1, c0)
+
+        d_planes = [held([P, PACK, M], F32, "dpl%d" % b) for b in range(HP)]
+        d_grouped = [held([P, PACK * M], BF16, "dg%d" % b) for b in range(HP)]
+
+        def first_stage(b, t):
+            cols = slice(t * P, (t + 1) * P)
+            h_banks, g_banks = [], []
+            for hf in range(S // BANK):
+                bank = psum.tile([P, BANK], F32, name="bank")
+                n = slice(hf * BANK, (hf + 1) * BANK)
+                for a in range(KP):
+                    nc.tensor.matmul_mx(
+                        out=bank[:],
+                        lhsT=w1_codes[a][b][:, cols].bitcast(FP8X4),
+                        lhsT_scale=w1_scales[a][b][:, cols],
+                        rhs=v_w[a][:, n].bitcast(FP8X4),
+                        rhs_scale=v_s[4 * a : P, n],
+                        start=(a == 0),
+                        stop=(a == KP - 1),
+                    )
+                h_banks.append(bank)
+            for hf in range(S // BANK):
+                bank = psum.tile([P, BANK], F32, name="bank")
+                n = slice(hf * BANK, (hf + 1) * BANK)
+                for a in range(KP):
+                    nc.tensor.matmul_mx(
+                        out=bank[:],
+                        lhsT=w2w[b][:, a, 2 * t * P : 2 * (t + 1) * P].bitcast(FP4X4),
+                        lhsT_scale=w2s[:, a, b * PASS + t * P : b * PASS + (t + 1) * P],
+                        rhs=v_w[a][:, n].bitcast(FP8X4),
+                        rhs_scale=(v_s, v_s1)[a][:, n],
+                        start=(a == 0),
+                        stop=(a == KP - 1),
+                    )
+                g_banks.append(bank)
+            h = two.tile([P, S], F32, name="h")
+            tops = two.tile([P, 2], F32, name="tops")
+            for hf in range(S // BANK):
+                nc.vector.tensor_scalar(
+                    h[:, hf * BANK : (hf + 1) * BANK], h_banks[hf][:], 1.0, None, ALU.mult, ALU.max,
+                    accum_out=tops[:, hf : hf + 1],
+                )
+            neg_top = two.tile([P, 1], F32, name="neg_top")
+            nc.gpsimd.tensor_scalar(neg_top[:], tops[:, 0:1], tops[:, 1:2], -1.0, ALU.max, ALU.mult)
+            look = two.tile([P, M], F32, name="look")
+            weight = three.tile([P, M], F32, name="weight")
+            parts = ((0, HALF), (HALF, M)) if (b, t) == (HP - 1, PACK - 1) else ((0, M),)
+            for m0, m1 in parts:
+                nc.scalar.activation(
+                    out=look[:, m0:m1], in_=h[:].indirect(pos1_t[:, m0 // 16 : m1 // 16]), func=ACT.Exp,
+                    bias=neg_top[:],
+                )
+                nc.scalar.activation(
+                    out=weight[:, m0:m1], in_=look[:, m0:m1], func=ACT.Copy,
+                    scale=gain_t[b][:, t : t + 1],
+                )
+            lead = three.tile([P, S], F32, name="lead")
+            for hf in range(S // BANK):
+                n = slice(hf * BANK, (hf + 1) * BANK)
+                nc.vector.tensor_tensor(lead[:, n], g_banks[hf][:], h[:, n], ALU.max)
+            return lead, weight
+
+        def pick(b, t, lead, weight, m0, m1):
+            nc.vector.tensor_tensor(
+                d_planes[b][:, t, m0:m1], lead[:].indirect(pos2_t[:, m0 // 16 : m1 // 16]), weight[:, m0:m1], ALU.mult
+            )
+
+        slices = [(b, t) for b in range(HP) for t in range(PACK)]
+        waiting = None
+        for i, (b, t) in enumerate(slices):
+            made = first_stage(b, t)
+            if waiting is not None:
+                pick(*waiting, 0, M)
+            waiting = (b, t) + made
+            if i == 0:
+                prepare_w1_b1(0)
+            if i == 1:
+                prepare_w1_b1(1)
+                deal_w2_words(1)
+            if i in (2, 3, 5, 6):
+                j = (2, 3, 5, 6).index(i)
+                prepare_w3(j // 2, j % 2)
+            if i == 4:
+                for m0 in (0, HALF):
+                    weave(nc.scalar.copy, d_grouped[0], d_planes[0], m0, m0 + HALF)
+                quantize(d_codes[0], d_scales[0], d_grouped[0], 0, M)
+
+        def second_pass(bank, u, b, m0):
+            for j in range(2):
+                cols = slice((2 * u + j) * P, (2 * u + j + 1) * P)
+                nc.tensor.matmul_mx(
+                    out=bank[:, j * HALF : (j + 1) * HALF],
+                    lhsT=w3_codes[b][:, cols].bitcast(FP8X4),
+                    lhsT_scale=w3_scales[b][:, cols],
+                    rhs=d_codes[b][:, m0 : m0 + HALF].bitcast(FP8X4),
+                    rhs_scale=d_scales[b][:, m0 : m0 + HALF],
+                    start=(b == 0 and j == 0),
+                    stop=(b == HP - 1 and j == 1),
+                )
+
+        pairs = N // (2 * P)
+        banks = {}
+        for m0 in (0, HALF):
+            for u in range(pairs):
+                banks[(m0, u)] = psum.tile([P, BANK], F32, name="bank")
+                second_pass(banks[(m0, u)], u, 0, m0)
+        for m0 in (0, HALF):
+            pick(*waiting, m0, m0 + HALF)
+            weave(nc.vector.tensor_copy, d_grouped[1], d_planes[1], m0, m0 + HALF)
+            quantize(d_codes[1], d_scales[1], d_grouped[1], m0, m0 + HALF)
+            for u in range(pairs):
+                second_pass(banks[(m0, u)], u, 1, m0)
+                result = held([P, BANK], F32, "result%d_%d" % (m0, u))
+                nc.scalar.activation(out=result[:], in_=banks[(m0, u)][:], func=ACT.Abs)
+                rows = out[2 * u * P : (2 * u + 2) * P, m0 : m0 + HALF]
+                nc.sync.dma_start(
+                    rows.rearrange("(j p) m -> p j m", p=P), result[:].rearrange("p (j m) -> p j m", j=2)
+                )

@@ -60,8 +60,8 @@ def tile_list_trisomy_bin_deviation_kernel(
         d_scales = [held([P, M], U8, "ds%d" % b) for b in range(HP)]
 
         nc.vector.memset(tab_s[:].bitcast(I32), 0)
-        nc.gpsimd.memset(w2s_raw[:].rearrange("p a n -> p (a n)").bitcast(I32), 0)
-        nc.gpsimd.memset(v_s1[:].bitcast(I32), 0)
+        nc.vector.memset(w2s_raw[:].rearrange("p a n -> p (a n)").bitcast(I32), 0)
+        nc.vector.memset(v_s1[:].bitcast(I32), 0)
 
         def load_tab_words(a):
             nc.sync.dma_start(tab_w[a][:], tab_words[a].rearrange("p t i -> p (t i)").bitcast(I32))
@@ -99,7 +99,7 @@ def tile_list_trisomy_bin_deviation_kernel(
         load_tab_words(0)
         ts32 = tab_scales.bitcast(I32)
         for q in range(4):
-            nc.sync.dma_start(tab_s[:].bitcast(I32)[32 * q : 32 * q + 4 * KP, :], ts32[:, 4 * q : 4 * q + 4, :])
+            nc.gpsimd.dma_start(tab_s[:].bitcast(I32)[32 * q : 32 * q + 4 * KP, :], ts32[:, 4 * q : 4 * q + 4, :])
         raw00 = load_w1(0, 0, 0, PASS, "w1raw00")
         load_tab_words(1)
         w2s32 = w2_scales.bitcast(I32)
@@ -115,7 +115,7 @@ def tile_list_trisomy_bin_deviation_kernel(
         nc.vector.tensor_copy(v_s[:], tab_s[:].indirect(offs_t[:]))
         nc.vector.tensor_copy(v_w[1][:], tab_w[1][:].bitcast(U32).indirect(offs_t[:]))
         for q in range(4):
-            nc.sync.dma_start(
+            nc.scalar.dma_start(
                 v_s1[:].bitcast(I32)[32 * q : 32 * q + 4, :], v_s[:].bitcast(I32)[32 * q + 4 : 32 * q + 8, :]
             )
         nc.sync.dma_start(pos1_t[:], pos1)
@@ -225,10 +225,15 @@ def tile_list_trisomy_bin_deviation_kernel(
                     out=look[:, m0:m1], in_=h[:].indirect(pos1_t[:, m0 // 16 : m1 // 16]), func=ACT.Exp,
                     bias=neg_top[:],
                 )
-                nc.scalar.activation(
-                    out=weight[:, m0:m1], in_=look[:, m0:m1], func=ACT.Copy,
-                    scale=gain_t[b][:, t : t + 1],
-                )
+                if len(parts) > 1:
+                    nc.scalar.activation(
+                        out=weight[:, m0:m1], in_=look[:, m0:m1], func=ACT.Copy,
+                        scale=gain_t[b][:, t : t + 1],
+                    )
+                else:
+                    nc.gpsimd.tensor_scalar(
+                        weight[:, m0:m1], look[:, m0:m1], gain_t[b][:, t : t + 1], 0.0, ALU.mult, ALU.add
+                    )
             lead = three.tile([P, S], F32, name="lead")
             for hf in range(S // BANK):
                 n = slice(hf * BANK, (hf + 1) * BANK)

@@ -23,6 +23,7 @@ BANK = 512
 KP = K // PASS
 HP = H // PASS
 HALF = M // 2
+SHARE = 192
 
 
 def tile_list_trisomy_bin_deviation_kernel(
@@ -32,8 +33,8 @@ def tile_list_trisomy_bin_deviation_kernel(
     with ExitStack() as ctx:
         keep = ctx.enter_context(tc.tile_pool(name="keep", bufs=1))
         two = ctx.enter_context(tc.tile_pool(name="two", bufs=2))
-        three = ctx.enter_context(tc.tile_pool(name="three", bufs=3))
-        psum = ctx.enter_context(tc.psum_pool(name="psum", bufs=8))
+        five = ctx.enter_context(tc.tile_pool(name="five", bufs=5))
+        psum = ctx.enter_context(tc.psum_pool(name="psum", bufs=1))
 
         def held(shape, dtype, name):
             return keep.tile(shape, dtype, name=name, align_bytes=64)
@@ -48,8 +49,7 @@ def tile_list_trisomy_bin_deviation_kernel(
         v_s = held([P, S], U8, "v_s")
         v_s1 = held([P, S], U8, "v_s1")
         w2s_raw = held([P, KP, H], U8, "w2s_raw")
-        w2s = held([P, KP, H], U8, "w2s")
-        w2w_raw = [held([P, KP, PASS // 2], I32, "w2w_raw%d" % b) for b in range(HP)]
+        w2w_raw = held([P, KP, H // 2], I32, "w2w_raw")
         w2w = [held([P, KP, 2 * PASS], U8, "w2w%d" % b) for b in range(HP)]
         gain_t = [held([P, PACK], F32, "gain_t%d" % b) for b in range(HP)]
         w1_codes = [[held([P, PASS], U32, "w1c%d%d" % (a, b)) for b in range(HP)] for a in range(KP)]
@@ -60,8 +60,8 @@ def tile_list_trisomy_bin_deviation_kernel(
         d_scales = [held([P, M], U8, "ds%d" % b) for b in range(HP)]
 
         nc.vector.memset(tab_s[:].bitcast(I32), 0)
-        nc.vector.memset(w2s_raw[:].rearrange("p a n -> p (a n)").bitcast(I32), 0)
-        nc.vector.memset(v_s1[:].bitcast(I32), 0)
+        nc.gpsimd.memset(w2s_raw[:].rearrange("p a n -> p (a n)").bitcast(I32), 0)
+        nc.gpsimd.memset(v_s1[:].bitcast(I32), 0)
 
         def load_tab_words(a):
             nc.sync.dma_start(tab_w[a][:], tab_words[a].rearrange("p t i -> p (t i)").bitcast(I32))
@@ -71,10 +71,6 @@ def tile_list_trisomy_bin_deviation_kernel(
             rows = w1[a * PASS : (a + 1) * PASS, b * PASS + c0 : b * PASS + c0 + width]
             nc.sync.dma_start(raw[:], rows.rearrange("(p j) c -> p j c", j=PACK))
             return raw
-
-        def load_w2_words(b):
-            src = w2_words.bitcast(I32)[:, :, b * (PASS // 2) : (b + 1) * (PASS // 2)]
-            nc.sync.dma_start(w2w_raw[b][:], src.rearrange("a p n -> p a n"))
 
         def weave_w1(copy, grouped, raw, r0, c0, width):
             w0, w1n = c0 // 16, (c0 + width) // 16
@@ -92,68 +88,74 @@ def tile_list_trisomy_bin_deviation_kernel(
         def deal_w2_words(b):
             for a in range(KP):
                 dst = w2w[b][:, a, :].bitcast(U32).rearrange("p (t w u) -> p w t u", t=PACK, u=2)
-                src = w2w_raw[b][:, a, :].bitcast(U32).rearrange("p (w t u) -> p w t u", t=PACK, u=2)
+                src = w2w_raw[:, a, b * (PASS // 2) : (b + 1) * (PASS // 2)].bitcast(U32).rearrange("p (w t u) -> p w t u", t=PACK, u=2)
                 nc.scalar.copy(dst, src)
+
+        def deal_w2_scales(w2s, b):
+            cols = slice(b * (PASS // 4), (b + 1) * (PASS // 4))
+            dst = w2s[:].bitcast(U32)[:, :, cols].rearrange("p a (t w) -> p a w t", t=PACK)
+            src = w2s_raw[:].bitcast(U32)[:, :, cols].rearrange("p a (w t) -> p a w t", t=PACK)
+            nc.scalar.copy(dst, src)
 
         nc.sync.dma_start(offs_t[:], offs)
         load_tab_words(0)
         ts32 = tab_scales.bitcast(I32)
         for q in range(4):
-            nc.gpsimd.dma_start(tab_s[:].bitcast(I32)[32 * q : 32 * q + 4 * KP, :], ts32[:, 4 * q : 4 * q + 4, :])
-        raw00 = load_w1(0, 0, 0, PASS, "w1raw00")
+            nc.sync.dma_start(tab_s[:].bitcast(I32)[32 * q : 32 * q + 4 * KP, :], ts32[:, 4 * q : 4 * q + 4, :])
+        raw_b0 = [load_w1(a, 0, 0, PASS, "w1raw%d" % a) for a in range(KP)]
         load_tab_words(1)
+        nc.sync.dma_start(w2w_raw[:], w2_words.bitcast(I32).rearrange("a p n -> p a n"))
         w2s32 = w2_scales.bitcast(I32)
         for q in range(4):
-            nc.sync.dma_start(
+            nc.gpsimd.dma_start(
                 w2s_raw[:].bitcast(I32)[32 * q : 32 * q + 4, :, :],
                 w2s32[:, 4 * q : 4 * q + 4, :].rearrange("a r n -> r a n"),
             )
-        raw10 = [load_w1(1, 0, c0, PASS // 2, "w1raw10_%d" % c0) for c0 in (0, PASS // 2)]
-        load_w2_words(0)
 
         nc.vector.tensor_copy(v_w[0][:], tab_w[0][:].bitcast(U32).indirect(offs_t[:]))
         nc.vector.tensor_copy(v_s[:], tab_s[:].indirect(offs_t[:]))
-        nc.vector.tensor_copy(v_w[1][:], tab_w[1][:].bitcast(U32).indirect(offs_t[:]))
         for q in range(4):
-            nc.scalar.dma_start(
+            nc.sync.dma_start(
                 v_s1[:].bitcast(I32)[32 * q : 32 * q + 4, :], v_s[:].bitcast(I32)[32 * q + 4 : 32 * q + 8, :]
             )
         nc.sync.dma_start(pos1_t[:], pos1)
         nc.sync.dma_start(pos2_t[:], pos2)
         gain_v = gain.rearrange("(b w t v) -> b v w t", b=HP, t=PACK, v=4)
 
-        def load_gain(b):
+        def load_gain(b, queue):
             with nc.allow_non_contiguous_dma(reason="one gain for each row of a slice"):
                 for v in range(4):
-                    nc.sync.dma_start(gain_t[b][v:P:4, :], gain_v[b, v])
+                    queue.dma_start(gain_t[b][v:P:4, :], gain_v[b, v])
 
-        load_gain(0)
+        load_gain(0, nc.gpsimd)
 
-        g00 = two.tile([P, PACK * PASS], BF16, name="w1g", align_bytes=64)
+        g00 = held([P, PACK * PASS], BF16, "first0")
         for c0 in (0, PASS // 2):
-            weave_w1(nc.scalar.copy, g00, raw00, c0, c0, PASS // 2)
+            weave_w1(nc.scalar.copy, g00, raw_b0[0], c0, c0, PASS // 2)
         quantize(w1_codes[0][0], w1_scales[0][0], g00, 0, PASS)
-        g10 = two.tile([P, PACK * PASS], BF16, name="w1g", align_bytes=64)
-        weave_w1(nc.scalar.copy, g10, raw10[0], 0, 0, PASS // 2)
-        weave_w1(nc.vector.tensor_copy, g10, raw10[1], 0, PASS // 2, PASS // 2)
-        quantize(w1_codes[1][0], w1_scales[1][0], g10, 0, P)
-        quantize(w1_codes[1][0], w1_scales[1][0], g10, P, PASS)
+        g10 = held([P, PACK * PASS], BF16, "first1")
+        weave_w1(nc.vector.tensor_copy, g10, raw_b0[1], 0, 0, PASS // 2)
+        weave_w1(nc.scalar.copy, g10, raw_b0[1], PASS // 2, PASS // 2, PASS // 2)
+        quantize(w1_codes[1][0], w1_scales[1][0], g10, 0, PASS)
+        for hf in range(S // BANK):
+            nc.vector.tensor_copy(
+                v_w[1][:, hf * BANK : (hf + 1) * BANK],
+                tab_w[1][:].bitcast(U32).indirect(offs_t[:, hf * (BANK // 16) : (hf + 1) * (BANK // 16)]),
+            )
+        w2s = held([P, KP, H], U8, "first0")
+        for b in range(HP):
+            deal_w2_words(b)
+            deal_w2_scales(w2s, b)
 
-        dst = w2s[:].rearrange("p a n -> p (a n)").bitcast(U32).rearrange("p (c t w) -> p c w t", t=PACK, w=32)
-        src = w2s_raw[:].rearrange("p a n -> p (a n)").bitcast(U32).rearrange("p (c w t) -> p c w t", t=PACK, w=32)
-        nc.scalar.copy(dst, src)
-        deal_w2_words(0)
-
-        raw_b1 = [load_w1(a, 1, 0, PASS, "w1raw%d1" % a) for a in range(KP)]
-        load_w2_words(1)
-        load_gain(1)
+        raw_b1 = [load_w1(a, 1, 0, PASS, "w1raw%d" % a) for a in range(KP)]
         w3_raw = []
         for b in range(HP):
-            raw = held([P, PACK, N], F32, "w3raw%d" % b)
+            raw = held([P, PACK, N], F32, ("first1", "w2w_raw")[b])
             rows = w3[b * PASS : (b + 1) * PASS, :].rearrange("(w t v) n -> t w v n", t=PACK, v=4)
             for t in range(PACK):
                 nc.sync.dma_start(raw[:, t, :], rows[t])
             w3_raw.append(raw)
+        load_gain(1, nc.sync)
 
         def prepare_w1_b1(a):
             grouped = two.tile([P, PACK * PASS], BF16, name="w1g", align_bytes=64)
@@ -161,9 +163,9 @@ def tile_list_trisomy_bin_deviation_kernel(
                 weave_w1(nc.scalar.copy, grouped, raw_b1[a], c0, c0, PASS // 2)
             quantize(w1_codes[a][1], w1_scales[a][1], grouped, 0, PASS)
 
-        def weave(copy, grouped, planes, c0, c1, g0=0):
+        def weave(copy, grouped, planes, c0, c1, g0=0, p0=0):
             dst = grouped[:, PACK * (c0 - g0) : PACK * (c1 - g0)].rearrange("p (c i t) -> p c t i", i=4, t=PACK)
-            src = planes[:, :, c0:c1].rearrange("p t (c i) -> p c t i", i=4)
+            src = planes[:, :, c0 - p0 : c1 - p0].rearrange("p t (c i) -> p c t i", i=4)
             copy(dst, src)
 
         def prepare_w3(b, part):
@@ -174,14 +176,14 @@ def tile_list_trisomy_bin_deviation_kernel(
             weave(nc.scalar.copy, grouped, w3_raw[b], mid, c1, c0)
             quantize(w3_codes[b], w3_scales[b], grouped, c0, c1, c0)
 
-        d_planes = [held([P, PACK, M], F32, "dpl%d" % b) for b in range(HP)]
-        d_grouped = [held([P, PACK * M], BF16, "dg%d" % b) for b in range(HP)]
+        d_planes = [held([P, PACK, M], F32, "dpl0"), held([P, PACK, HALF], F32, "dpl1")]
+        d_grouped = [held([P, PACK * M], BF16, "dg0")]
 
         def first_stage(b, t):
             cols = slice(t * P, (t + 1) * P)
             h_banks, g_banks = [], []
             for hf in range(S // BANK):
-                bank = psum.tile([P, BANK], F32, name="bank")
+                bank = psum.tile([P, BANK], F32, name="bank%d" % (4 * (t % 2) + hf))
                 n = slice(hf * BANK, (hf + 1) * BANK)
                 for a in range(KP):
                     nc.tensor.matmul_mx(
@@ -195,7 +197,7 @@ def tile_list_trisomy_bin_deviation_kernel(
                     )
                 h_banks.append(bank)
             for hf in range(S // BANK):
-                bank = psum.tile([P, BANK], F32, name="bank")
+                bank = psum.tile([P, BANK], F32, name="bank%d" % (4 * (t % 2) + 2 + hf))
                 n = slice(hf * BANK, (hf + 1) * BANK)
                 for a in range(KP):
                     nc.tensor.matmul_mx(
@@ -208,6 +210,7 @@ def tile_list_trisomy_bin_deviation_kernel(
                         stop=(a == KP - 1),
                     )
                 g_banks.append(bank)
+            last = (b, t) == (HP - 1, PACK - 1)
             h = two.tile([P, S], F32, name="h")
             tops = two.tile([P, 2], F32, name="tops")
             for hf in range(S // BANK):
@@ -217,46 +220,45 @@ def tile_list_trisomy_bin_deviation_kernel(
                 )
             neg_top = two.tile([P, 1], F32, name="neg_top")
             nc.gpsimd.tensor_scalar(neg_top[:], tops[:, 0:1], tops[:, 1:2], -1.0, ALU.max, ALU.mult)
-            look = two.tile([P, M], F32, name="look")
-            weight = three.tile([P, M], F32, name="weight")
-            parts = ((0, HALF), (HALF, M)) if (b, t) == (HP - 1, PACK - 1) else ((0, M),)
-            for m0, m1 in parts:
-                nc.scalar.activation(
-                    out=look[:, m0:m1], in_=h[:].indirect(pos1_t[:, m0 // 16 : m1 // 16]), func=ACT.Exp,
-                    bias=neg_top[:],
-                )
-                if len(parts) > 1:
+            if last:
+                weight = []
+                for m0 in (0, HALF):
+                    look = held([P, HALF], F32, "look_last")
+                    part = held([P, HALF], F32, "late" if m0 == 0 else "weight_last")
                     nc.scalar.activation(
-                        out=weight[:, m0:m1], in_=look[:, m0:m1], func=ACT.Copy,
-                        scale=gain_t[b][:, t : t + 1],
+                        out=look[:], in_=h[:].indirect(pos1_t[:, m0 // 16 : (m0 + HALF) // 16]), func=ACT.Exp,
+                        bias=neg_top[:],
                     )
-                else:
-                    nc.gpsimd.tensor_scalar(
-                        weight[:, m0:m1], look[:, m0:m1], gain_t[b][:, t : t + 1], 0.0, ALU.mult, ALU.add
-                    )
-            lead = three.tile([P, S], F32, name="lead")
+                    nc.scalar.activation(out=part[:], in_=look[:], func=ACT.Copy, scale=gain_t[b][:, t : t + 1])
+                    weight.append(part[:])
+            else:
+                look = two.tile([P, M], F32, name="look")
+                whole = five.tile([P, M], F32, name="weight")
+                nc.scalar.activation(out=look[:], in_=h[:].indirect(pos1_t[:]), func=ACT.Exp, bias=neg_top[:])
+                nc.gpsimd.tensor_scalar(whole[:], look[:], gain_t[b][:, t : t + 1], 0.0, ALU.mult, ALU.add)
+                weight = [whole[:, 0:HALF], whole[:, HALF:M], whole[:]]
+            lead = five.tile([P, S], F32, name="lead")
             for hf in range(S // BANK):
                 n = slice(hf * BANK, (hf + 1) * BANK)
                 nc.vector.tensor_tensor(lead[:, n], g_banks[hf][:], h[:, n], ALU.max)
             return lead, weight
 
-        def pick(b, t, lead, weight, m0, m1):
+        def pick(b, t, lead, weight, m0, m1, planes, p0):
             nc.vector.tensor_tensor(
-                d_planes[b][:, t, m0:m1], lead[:].indirect(pos2_t[:, m0 // 16 : m1 // 16]), weight[:, m0:m1], ALU.mult
+                planes[:, t, m0 - p0 : m1 - p0], lead[:].indirect(pos2_t[:, m0 // 16 : m1 // 16]), weight[2 if m1 - m0 == M else m0 // HALF], ALU.mult
             )
 
         slices = [(b, t) for b in range(HP) for t in range(PACK)]
-        waiting = None
+        made = []
         for i, (b, t) in enumerate(slices):
-            made = first_stage(b, t)
-            if waiting is not None:
-                pick(*waiting, 0, M)
-            waiting = (b, t) + made
+            made.append((b, t) + first_stage(b, t))
+            if i > 0:
+                before = made[i - 1]
+                pick(*before, 0, M if before[0] < HP - 1 else HALF, d_planes[before[0]], 0)
             if i == 0:
                 prepare_w1_b1(0)
             if i == 1:
                 prepare_w1_b1(1)
-                deal_w2_words(1)
             if i in (2, 3, 5, 6):
                 j = (2, 3, 5, 6).index(i)
                 prepare_w3(j // 2, j % 2)
@@ -282,12 +284,11 @@ def tile_list_trisomy_bin_deviation_kernel(
         banks = {}
         for m0 in (0, HALF):
             for u in range(pairs):
-                banks[(m0, u)] = psum.tile([P, BANK], F32, name="bank")
+                banks[(m0, u)] = psum.tile([P, BANK], F32, name="bank%d" % (u if m0 == 0 else 5 + u))
                 second_pass(banks[(m0, u)], u, 0, m0)
-        for m0 in (0, HALF):
-            pick(*waiting, m0, m0 + HALF)
-            weave(nc.vector.tensor_copy, d_grouped[1], d_planes[1], m0, m0 + HALF)
-            quantize(d_codes[1], d_scales[1], d_grouped[1], m0, m0 + HALF)
+
+        def finish(m0, grouped):
+            quantize(d_codes[1], d_scales[1], grouped, m0, m0 + HALF, m0)
             for u in range(pairs):
                 second_pass(banks[(m0, u)], u, 1, m0)
                 result = held([P, BANK], F32, "result%d_%d" % (m0, u))
@@ -296,3 +297,15 @@ def tile_list_trisomy_bin_deviation_kernel(
                 nc.sync.dma_start(
                     rows.rearrange("(j p) m -> p j m", p=P), result[:].rearrange("p (j m) -> p j m", j=2)
                 )
+
+        pick(*made[-1], 0, HALF, d_planes[1], 0)
+        grouped = held([P, PACK * HALF], BF16, "dg1")
+        weave(nc.scalar.copy, grouped, d_planes[1], 0, SHARE)
+        weave(nc.vector.tensor_copy, grouped, d_planes[1], SHARE, HALF)
+        finish(0, grouped)
+        late_planes = held([P, PACK, HALF], F32, "late")
+        for each in made[PACK:]:
+            pick(*each, HALF, M, late_planes, HALF)
+        grouped = held([P, PACK * HALF], BF16, "dg1")
+        weave(nc.vector.tensor_copy, grouped, late_planes, HALF, M, HALF, HALF)
+        finish(HALF, grouped)

@@ -23,7 +23,8 @@ BANK = 512
 KP = K // PASS
 HP = H // PASS
 HALF = M // 2
-SHARE = 192
+SHARE = 160
+HEAD_SHARE = 320
 
 
 def tile_list_trisomy_bin_deviation_kernel(
@@ -127,15 +128,14 @@ def tile_list_trisomy_bin_deviation_kernel(
                 for v in range(4):
                     queue.dma_start(gain_t[b][v:P:4, :], gain_v[b, v])
 
-        load_gain(0, nc.gpsimd)
 
         g00 = held([P, PACK * PASS], BF16, "first0")
         for c0 in (0, PASS // 2):
             weave_w1(nc.scalar.copy, g00, raw_b0[0], c0, c0, PASS // 2)
         quantize(w1_codes[0][0], w1_scales[0][0], g00, 0, PASS)
         g10 = held([P, PACK * PASS], BF16, "first1")
-        weave_w1(nc.vector.tensor_copy, g10, raw_b0[1], 0, 0, PASS // 2)
-        weave_w1(nc.scalar.copy, g10, raw_b0[1], PASS // 2, PASS // 2, PASS // 2)
+        weave_w1(nc.vector.tensor_copy, g10, raw_b0[1], 0, 0, HEAD_SHARE)
+        weave_w1(nc.scalar.copy, g10, raw_b0[1], HEAD_SHARE, HEAD_SHARE, PASS - HEAD_SHARE)
         quantize(w1_codes[1][0], w1_scales[1][0], g10, 0, PASS)
         for hf in range(S // BANK):
             nc.vector.tensor_copy(
@@ -148,6 +148,7 @@ def tile_list_trisomy_bin_deviation_kernel(
             deal_w2_scales(w2s, b)
 
         raw_b1 = [load_w1(a, 1, 0, PASS, "w1raw%d" % a) for a in range(KP)]
+        load_gain(0, nc.sync)
         w3_raw = []
         for b in range(HP):
             raw = held([P, PACK, N], F32, ("first1", "w2w_raw")[b])
@@ -221,7 +222,7 @@ def tile_list_trisomy_bin_deviation_kernel(
             neg_top = two.tile([P, 1], F32, name="neg_top")
             nc.gpsimd.tensor_scalar(neg_top[:], tops[:, 0:1], tops[:, 1:2], -1.0, ALU.max, ALU.mult)
             if last:
-                weight = []
+                halves = []
                 for m0 in (0, HALF):
                     look = held([P, HALF], F32, "look_last")
                     part = held([P, HALF], F32, "late" if m0 == 0 else "weight_last")
@@ -230,13 +231,14 @@ def tile_list_trisomy_bin_deviation_kernel(
                         bias=neg_top[:],
                     )
                     nc.scalar.activation(out=part[:], in_=look[:], func=ACT.Copy, scale=gain_t[b][:, t : t + 1])
-                    weight.append(part[:])
+                    halves.append(part)
+                weight = lambda m0, m1: halves[m0 // HALF][:, m0 % HALF : m1 - m0 + m0 % HALF]
             else:
                 look = two.tile([P, M], F32, name="look")
                 whole = five.tile([P, M], F32, name="weight")
                 nc.scalar.activation(out=look[:], in_=h[:].indirect(pos1_t[:]), func=ACT.Exp, bias=neg_top[:])
-                nc.gpsimd.tensor_scalar(whole[:], look[:], gain_t[b][:, t : t + 1], 0.0, ALU.mult, ALU.add)
-                weight = [whole[:, 0:HALF], whole[:, HALF:M], whole[:]]
+                nc.scalar.activation(out=whole[:], in_=look[:], func=ACT.Copy, scale=gain_t[b][:, t : t + 1])
+                weight = lambda m0, m1: whole[:, m0:m1]
             lead = five.tile([P, S], F32, name="lead")
             for hf in range(S // BANK):
                 n = slice(hf * BANK, (hf + 1) * BANK)
@@ -245,7 +247,7 @@ def tile_list_trisomy_bin_deviation_kernel(
 
         def pick(b, t, lead, weight, m0, m1, planes, p0):
             nc.vector.tensor_tensor(
-                planes[:, t, m0 - p0 : m1 - p0], lead[:].indirect(pos2_t[:, m0 // 16 : m1 // 16]), weight[2 if m1 - m0 == M else m0 // HALF], ALU.mult
+                planes[:, t, m0 - p0 : m1 - p0], lead[:].indirect(pos2_t[:, m0 // 16 : m1 // 16]), weight(m0, m1), ALU.mult
             )
 
         slices = [(b, t) for b in range(HP) for t in range(PACK)]
@@ -267,35 +269,46 @@ def tile_list_trisomy_bin_deviation_kernel(
                     weave(nc.scalar.copy, d_grouped[0], d_planes[0], m0, m0 + HALF)
                 quantize(d_codes[0], d_scales[0], d_grouped[0], 0, M)
 
-        def second_pass(bank, u, b, m0):
-            for j in range(2):
-                cols = slice((2 * u + j) * P, (2 * u + j + 1) * P)
+        parts = [(0, HALF), (HALF, HALF + P), (HALF + P, M)]
+        bank_names = [(0, 1, 2), (3, 4), (6, 7)]
+
+        def second_pass(bank, tiles, b, m0, m1):
+            width = m1 - m0
+            for j, n_tile in enumerate(tiles):
+                cols = slice(n_tile * P, (n_tile + 1) * P)
                 nc.tensor.matmul_mx(
-                    out=bank[:, j * HALF : (j + 1) * HALF],
+                    out=bank[:, j * width : (j + 1) * width],
                     lhsT=w3_codes[b][:, cols].bitcast(FP8X4),
                     lhsT_scale=w3_scales[b][:, cols],
-                    rhs=d_codes[b][:, m0 : m0 + HALF].bitcast(FP8X4),
-                    rhs_scale=d_scales[b][:, m0 : m0 + HALF],
+                    rhs=d_codes[b][:, m0:m1].bitcast(FP8X4),
+                    rhs_scale=d_scales[b][:, m0:m1],
                     start=(b == 0 and j == 0),
-                    stop=(b == HP - 1 and j == 1),
+                    stop=(b == HP - 1 and j == len(tiles) - 1),
                 )
 
-        pairs = N // (2 * P)
-        banks = {}
-        for m0 in (0, HALF):
-            for u in range(pairs):
-                banks[(m0, u)] = psum.tile([P, BANK], F32, name="bank%d" % (u if m0 == 0 else 5 + u))
-                second_pass(banks[(m0, u)], u, 0, m0)
+        groups = []
+        for (m0, m1), names in zip(parts, bank_names):
+            per_bank = (N // P) // len(names)
+            group = []
+            for u, name in enumerate(names):
+                bank = psum.tile([P, BANK], F32, name="bank%d" % name)
+                tiles = list(range(u * per_bank, (u + 1) * per_bank))
+                second_pass(bank, tiles, 0, m0, m1)
+                group.append((bank, tiles))
+            groups.append(group)
 
-        def finish(m0, grouped):
-            quantize(d_codes[1], d_scales[1], grouped, m0, m0 + HALF, m0)
-            for u in range(pairs):
-                second_pass(banks[(m0, u)], u, 1, m0)
-                result = held([P, BANK], F32, "result%d_%d" % (m0, u))
-                nc.scalar.activation(out=result[:], in_=banks[(m0, u)][:], func=ACT.Abs)
-                rows = out[2 * u * P : (2 * u + 2) * P, m0 : m0 + HALF]
+        def finish(part, grouped):
+            m0, m1 = parts[part]
+            width = m1 - m0
+            quantize(d_codes[1], d_scales[1], grouped, m0, m1, m0)
+            for bank, tiles in groups[part]:
+                second_pass(bank, tiles, 1, m0, m1)
+                used = len(tiles) * width
+                result = held([P, used], F32, "result%d_%d" % (m0, tiles[0]))
+                nc.scalar.activation(out=result[:], in_=bank[:, 0:used], func=ACT.Abs)
+                rows = out[tiles[0] * P : (tiles[-1] + 1) * P, m0:m1]
                 nc.sync.dma_start(
-                    rows.rearrange("(j p) m -> p j m", p=P), result[:].rearrange("p (j m) -> p j m", j=2)
+                    rows.rearrange("(j p) m -> p j m", p=P), result[:].rearrange("p (j m) -> p j m", m=width)
                 )
 
         pick(*made[-1], 0, HALF, d_planes[1], 0)
@@ -303,9 +316,11 @@ def tile_list_trisomy_bin_deviation_kernel(
         weave(nc.scalar.copy, grouped, d_planes[1], 0, SHARE)
         weave(nc.vector.tensor_copy, grouped, d_planes[1], SHARE, HALF)
         finish(0, grouped)
-        late_planes = held([P, PACK, HALF], F32, "late")
-        for each in made[PACK:]:
-            pick(*each, HALF, M, late_planes, HALF)
-        grouped = held([P, PACK * HALF], BF16, "dg1")
-        weave(nc.vector.tensor_copy, grouped, late_planes, HALF, M, HALF, HALF)
-        finish(HALF, grouped)
+        for part, name in ((1, "late"), (2, "dg1")):
+            m0, m1 = parts[part]
+            planes = held([P, PACK, P], F32, name)
+            for each in made[PACK:]:
+                pick(*each, m0, m1, planes, m0)
+            grouped = held([P, PACK * P], BF16, "dg_late%d" % part)
+            weave(nc.vector.tensor_copy, grouped, planes, m0, m1, m0, m0)
+            finish(part, grouped)

from contextlib import ExitStack

import concourse.mybir as mybir

K, H, N, T, S, M = 1024, 1024, 768, 2048, 1024, 512
FLOPS = 2 * K * H * S * 2 + 2 * H * N * M

F32 = mybir.dt.float32
BF16 = mybir.dt.bfloat16
I32 = mybir.dt.int32
U32 = mybir.dt.uint32
U16 = mybir.dt.uint16
U8 = mybir.dt.uint8
FP8X4 = mybir.dt.float8_e4m3fn_x4
FP4X4 = mybir.dt.float4_e2m1fn_x4
ALU = mybir.AluOpType
ACT = mybir.ActivationFunctionType

P = 128
PACK = 4
PASS = P * PACK
BANK = 512
KP = K // PASS
HP = H // PASS
HALF = M // 2
SHARE = 160
HEAD_SHARE = 320


def tile_list_trisomy_bin_deviation_kernel(
    tc, tab_words, tab_scales, offs, pos1, pos2, w1, w2_words, w2_scales, gain, w3, out
):
    nc = tc.nc
    with ExitStack() as ctx:
        keep = ctx.enter_context(tc.tile_pool(name="keep", bufs=1))
        two = ctx.enter_context(tc.tile_pool(name="two", bufs=2))
        five = ctx.enter_context(tc.tile_pool(name="five", bufs=5))
        psum = ctx.enter_context(tc.psum_pool(name="psum", bufs=1))

        def held(shape, dtype, name):
            return keep.tile(shape, dtype, name=name, align_bytes=64)

        offs_t = keep.tile([P, S // 16], U16, name="offs_t")
        pos1_t = keep.tile([P, M // 16], U16, name="pos1_t")
        pos2_t = keep.tile([P, M // 16], U16, name="pos2_t")

        tab_w = [held([P, T], I32, "tab_w%d" % a) for a in range(KP)]
        tab_s = held([P, T], U8, "tab_s")
        v_w = [held([P, S], U32, "v_w%d" % a) for a in range(KP)]
        v_s = held([P, S], U8, "v_s")
        v_s1 = held([P, S], U8, "v_s1")
        w2s_raw = held([P, KP, H], U8, "w2s_raw")
        w2w_raw = held([P, KP, H // 2], I32, "w2w_raw")
        w2w = [held([P, KP, 2 * PASS], U8, "w2w%d" % b) for b in range(HP)]
        gain_t = [held([P, PACK], F32, "gain_t%d" % b) for b in range(HP)]
        w1_codes = [[held([P, PASS], U32, "w1c%d%d" % (a, b)) for b in range(HP)] for a in range(KP)]
        w1_scales = [[held([P, PASS], U8, "w1s%d%d" % (a, b)) for b in range(HP)] for a in range(KP)]
        w3_codes = [held([P, N], U32, "w3c%d" % b) for b in range(HP)]
        w3_scales = [held([P, N], U8, "w3s%d" % b) for b in range(HP)]
        d_codes = [held([P, M], U32, "dc%d" % b) for b in range(HP)]
        d_scales = [held([P, M], U8, "ds%d" % b) for b in range(HP)]

        nc.vector.memset(tab_s[:].bitcast(I32), 0)
        nc.gpsimd.memset(w2s_raw[:].rearrange("p a n -> p (a n)").bitcast(I32), 0)
        nc.gpsimd.memset(v_s1[:].bitcast(I32), 0)

        def load_tab_words(a):
            nc.sync.dma_start(tab_w[a][:], tab_words[a].rearrange("p t i -> p (t i)").bitcast(I32))

        def load_w1(a, b, c0, width, name):
            raw = held([P, PACK, width], F32, name)
            rows = w1[a * PASS : (a + 1) * PASS, b * PASS + c0 : b * PASS + c0 + width]
            nc.sync.dma_start(raw[:], rows.rearrange("(p j) c -> p j c", j=PACK))
            return raw

        def weave_w1(copy, grouped, raw, r0, c0, width):
            w0, w1n = c0 // 16, (c0 + width) // 16
            dst = grouped[:].rearrange("p (t w v j) -> p w t j v", t=PACK, v=4, j=PACK)[:, w0:w1n]
            src = raw[:, :, r0 : r0 + width].rearrange("p j (w t v) -> p w t j v", t=PACK, v=4)
            copy(dst, src)

        def quantize(codes, scales, grouped, c0, c1, g0=0):
            nc.vector.quantize_mx(
                out=codes[:, c0:c1].bitcast(FP8X4),
                scales=scales[:, c0:c1],
                in_=grouped[:, PACK * (c0 - g0) : PACK * (c1 - g0)],
            )

        def deal_w2_words(b):
            for a in range(KP):
                dst = w2w[b][:, a, :].bitcast(U32).rearrange("p (t w u) -> p w t u", t=PACK, u=2)
                src = w2w_raw[:, a, b * (PASS // 2) : (b + 1) * (PASS // 2)].bitcast(U32).rearrange("p (w t u) -> p w t u", t=PACK, u=2)
                nc.scalar.copy(dst, src)

        def deal_w2_scales(w2s, b):
            cols = slice(b * (PASS // 4), (b + 1) * (PASS // 4))
            dst = w2s[:].bitcast(U32)[:, :, cols].rearrange("p a (t w) -> p a w t", t=PACK)
            src = w2s_raw[:].bitcast(U32)[:, :, cols].rearrange("p a (w t) -> p a w t", t=PACK)
            nc.scalar.copy(dst, src)

        nc.sync.dma_start(offs_t[:], offs)
        load_tab_words(0)
        ts32 = tab_scales.bitcast(I32)
        for q in range(4):
            nc.sync.dma_start(tab_s[:].bitcast(I32)[32 * q : 32 * q + 4 * KP, :], ts32[:, 4 * q : 4 * q + 4, :])
        raw_b0 = [load_w1(a, 0, 0, PASS, "w1raw%d" % a) for a in range(KP)]
        load_tab_words(1)
        nc.sync.dma_start(w2w_raw[:], w2_words.bitcast(I32).rearrange("a p n -> p a n"))
        w2s32 = w2_scales.bitcast(I32)
        for q in range(4):
            nc.gpsimd.dma_start(
                w2s_raw[:].bitcast(I32)[32 * q : 32 * q + 4, :, :],
                w2s32[:, 4 * q : 4 * q + 4, :].rearrange("a r n -> r a n"),
            )

        nc.vector.tensor_copy(v_w[0][:], tab_w[0][:].bitcast(U32).indirect(offs_t[:]))
        nc.vector.tensor_copy(v_s[:], tab_s[:].indirect(offs_t[:]))
        for q in range(4):
            nc.sync.dma_start(
                v_s1[:].bitcast(I32)[32 * q : 32 * q + 4, :], v_s[:].bitcast(I32)[32 * q + 4 : 32 * q + 8, :]
            )
        nc.sync.dma_start(pos1_t[:], pos1)
        nc.sync.dma_start(pos2_t[:], pos2)
        gain_v = gain.rearrange("(b w t v) -> b v w t", b=HP, t=PACK, v=4)

        def load_gain(b, queue):
            with nc.allow_non_contiguous_dma(reason="one gain for each row of a slice"):
                for v in range(4):
                    queue.dma_start(gain_t[b][v:P:4, :], gain_v[b, v])


        g00 = held([P, PACK * PASS], BF16, "first0")
        for c0 in (0, PASS // 2):
            weave_w1(nc.scalar.copy, g00, raw_b0[0], c0, c0, PASS // 2)
        quantize(w1_codes[0][0], w1_scales[0][0], g00, 0, PASS)
        g10 = held([P, PACK * PASS], BF16, "first1")
        weave_w1(nc.vector.tensor_copy, g10, raw_b0[1], 0, 0, HEAD_SHARE)
        weave_w1(nc.scalar.copy, g10, raw_b0[1], HEAD_SHARE, HEAD_SHARE, PASS - HEAD_SHARE)
        quantize(w1_codes[1][0], w1_scales[1][0], g10, 0, PASS)
        for hf in range(S // BANK):
            nc.vector.tensor_copy(
                v_w[1][:, hf * BANK : (hf + 1) * BANK],
                tab_w[1][:].bitcast(U32).indirect(offs_t[:, hf * (BANK // 16) : (hf + 1) * (BANK // 16)]),
            )
        w2s = held([P, KP, H], U8, "first0")
        for b in range(HP):
            deal_w2_words(b)
            deal_w2_scales(w2s, b)

        raw_b1 = [load_w1(a, 1, 0, PASS, "w1raw%d" % a) for a in range(KP)]
        load_gain(0, nc.sync)
        w3_raw = []
        for b in range(HP):
            raw = held([P, PACK, N], F32, ("first1", "w2w_raw")[b])
            rows = w3[b * PASS : (b + 1) * PASS, :].rearrange("(w t v) n -> t w v n", t=PACK, v=4)
            for t in range(PACK):
                nc.sync.dma_start(raw[:, t, :], rows[t])
            w3_raw.append(raw)
        load_gain(1, nc.sync)

        def prepare_w1_b1(a):
            grouped = two.tile([P, PACK * PASS], BF16, name="w1g", align_bytes=64)
            for c0 in (0, PASS // 2):
                weave_w1(nc.scalar.copy, grouped, raw_b1[a], c0, c0, PASS // 2)
            quantize(w1_codes[a][1], w1_scales[a][1], grouped, 0, PASS)

        def weave(copy, grouped, planes, c0, c1, g0=0, p0=0):
            dst = grouped[:, PACK * (c0 - g0) : PACK * (c1 - g0)].rearrange("p (c i t) -> p c t i", i=4, t=PACK)
            src = planes[:, :, c0 - p0 : c1 - p0].rearrange("p t (c i) -> p c t i", i=4)
            copy(dst, src)

        def prepare_w3(b, part):
            c0, c1 = part * (N // 2), (part + 1) * (N // 2)
            grouped = two.tile([P, PACK * (N // 2)], BF16, name="w3g", align_bytes=64)
            mid = (c0 + c1) // 2
            weave(nc.scalar.copy, grouped, w3_raw[b], c0, mid, c0)
            weave(nc.scalar.copy, grouped, w3_raw[b], mid, c1, c0)
            quantize(w3_codes[b], w3_scales[b], grouped, c0, c1, c0)

        d_planes = [held([P, PACK, M], F32, "dpl0"), held([P, PACK, HALF], F32, "dpl1")]
        d_grouped = [held([P, PACK * M], BF16, "dg0")]

        def first_stage(b, t):
            cols = slice(t * P, (t + 1) * P)
            h_banks, g_banks = [], []
            for hf in range(S // BANK):
                bank = psum.tile([P, BANK], F32, name="bank%d" % (4 * (t % 2) + hf))
                n = slice(hf * BANK, (hf + 1) * BANK)
                for a in range(KP):
                    nc.tensor.matmul_mx(
                        out=bank[:],
                        lhsT=w1_codes[a][b][:, cols].bitcast(FP8X4),
                        lhsT_scale=w1_scales[a][b][:, cols],
                        rhs=v_w[a][:, n].bitcast(FP8X4),
                        rhs_scale=v_s[4 * a : P, n],
                        start=(a == 0),
                        stop=(a == KP - 1),
                    )
                h_banks.append(bank)
            for hf in range(S // BANK):
                bank = psum.tile([P, BANK], F32, name="bank%d" % (4 * (t % 2) + 2 + hf))
                n = slice(hf * BANK, (hf + 1) * BANK)
                for a in range(KP):
                    nc.tensor.matmul_mx(
                        out=bank[:],
                        lhsT=w2w[b][:, a, 2 * t * P : 2 * (t + 1) * P].bitcast(FP4X4),
                        lhsT_scale=w2s[:, a, b * PASS + t * P : b * PASS + (t + 1) * P],
                        rhs=v_w[a][:, n].bitcast(FP8X4),
                        rhs_scale=(v_s, v_s1)[a][:, n],
                        start=(a == 0),
                        stop=(a == KP - 1),
                    )
                g_banks.append(bank)
            last = (b, t) == (HP - 1, PACK - 1)
            h = two.tile([P, S], F32, name="h")
            tops = two.tile([P, 2], F32, name="tops")
            for hf in range(S // BANK):
                nc.vector.tensor_scalar(
                    h[:, hf * BANK : (hf + 1) * BANK], h_banks[hf][:], 1.0, None, ALU.mult, ALU.max,
                    accum_out=tops[:, hf : hf + 1],
                )
            neg_top = two.tile([P, 1], F32, name="neg_top")
            nc.gpsimd.tensor_scalar(neg_top[:], tops[:, 0:1], tops[:, 1:2], -1.0, ALU.max, ALU.mult)
            if last:
                halves = []
                for m0 in (0, HALF):
                    look = held([P, HALF], F32, "look_last")
                    part = held([P, HALF], F32, "late" if m0 == 0 else "weight_last")
                    nc.scalar.activation(
                        out=look[:], in_=h[:].indirect(pos1_t[:, m0 // 16 : (m0 + HALF) // 16]), func=ACT.Exp,
                        bias=neg_top[:],
                    )
                    nc.scalar.activation(out=part[:], in_=look[:], func=ACT.Copy, scale=gain_t[b][:, t : t + 1])
                    halves.append(part)
                weight = lambda m0, m1: halves[m0 // HALF][:, m0 % HALF : m1 - m0 + m0 % HALF]
            else:
                look = two.tile([P, M], F32, name="look")
                whole = five.tile([P, M], F32, name="weight")
                nc.scalar.activation(out=look[:], in_=h[:].indirect(pos1_t[:]), func=ACT.Exp, bias=neg_top[:])
                nc.scalar.activation(out=whole[:], in_=look[:], func=ACT.Copy, scale=gain_t[b][:, t : t + 1])
                weight = lambda m0, m1: whole[:, m0:m1]
            lead = five.tile([P, S], F32, name="lead")
            for hf in range(S // BANK):
                n = slice(hf * BANK, (hf + 1) * BANK)
                nc.vector.tensor_tensor(lead[:, n], g_banks[hf][:], h[:, n], ALU.max)
            return lead, weight

        def pick(b, t, lead, weight, m0, m1, planes, p0):
            nc.vector.tensor_tensor(
                planes[:, t, m0 - p0 : m1 - p0], lead[:].indirect(pos2_t[:, m0 // 16 : m1 // 16]), weight(m0, m1), ALU.mult
            )

        slices = [(b, t) for b in range(HP) for t in range(PACK)]
        made = []
        for i, (b, t) in enumerate(slices):
            made.append((b, t) + first_stage(b, t))
            if i > 0:
                before = made[i - 1]
                pick(*before, 0, M if before[0] < HP - 1 else HALF, d_planes[before[0]], 0)
            if i == 0:
                prepare_w1_b1(0)
            if i == 1:
                prepare_w1_b1(1)
            if i in (2, 3, 5, 6):
                j = (2, 3, 5, 6).index(i)
                prepare_w3(j // 2, j % 2)
            if i == 4:
                for m0 in (0, HALF):
                    weave(nc.scalar.copy, d_grouped[0], d_planes[0], m0, m0 + HALF)
                quantize(d_codes[0], d_scales[0], d_grouped[0], 0, M)

        parts = [(0, HALF), (HALF, HALF + P), (HALF + P, M)]
        bank_names = [(0, 1, 2), (3, 4), (6, 7)]

        def second_pass(bank, tiles, b, m0, m1):
            width = m1 - m0
            for j, n_tile in enumerate(tiles):
                cols = slice(n_tile * P, (n_tile + 1) * P)
                nc.tensor.matmul_mx(
                    out=bank[:, j * width : (j + 1) * width],
                    lhsT=w3_codes[b][:, cols].bitcast(FP8X4),
                    lhsT_scale=w3_scales[b][:, cols],
                    rhs=d_codes[b][:, m0:m1].bitcast(FP8X4),
                    rhs_scale=d_scales[b][:, m0:m1],
                    start=(b == 0 and j == 0),
                    stop=(b == HP - 1 and j == len(tiles) - 1),
                )

        groups = []
        for (m0, m1), names in zip(parts, bank_names):
            per_bank = (N // P) // len(names)
            group = []
            for u, name in enumerate(names):
                bank = psum.tile([P, BANK], F32, name="bank%d" % name)
                tiles = list(range(u * per_bank, (u + 1) * per_bank))
                second_pass(bank, tiles, 0, m0, m1)
                group.append((bank, tiles))
            groups.append(group)

        def finish(part, grouped):
            m0, m1 = parts[part]
            width = m1 - m0
            quantize(d_codes[1], d_scales[1], grouped, m0, m1, m0)
            for bank, tiles in groups[part]:
                second_pass(bank, tiles, 1, m0, m1)
                used = len(tiles) * width
                result = held([P, used], F32, "result%d_%d" % (m0, tiles[0]))
                nc.scalar.activation(out=result[:], in_=bank[:, 0:used], func=ACT.Abs)
                rows = out[tiles[0] * P : (tiles[-1] + 1) * P, m0:m1]
                nc.sync.dma_start(
                    rows.rearrange("(j p) m -> p j m", p=P), result[:].rearrange("p (j m) -> p j m", m=width)
                )

        pick(*made[-1], 0, HALF, d_planes[1], 0)
        grouped = held([P, PACK * HALF], BF16, "dg1")
        weave(nc.scalar.copy, grouped, d_planes[1], 0, SHARE)
        weave(nc.vector.tensor_copy, grouped, d_planes[1], SHARE, HALF)
        finish(0, grouped)
        for part, name in ((1, "late"), (2, "dg1")):
            m0, m1 = parts[part]
            planes = held([P, PACK, P], F32, name)
            for each in made[PACK:]:
                pick(*each, m0, m1, planes, m0)
            grouped = held([P, PACK * P], BF16, "dg_late%d" % part)
            weave(nc.vector.tensor_copy, grouped, planes, m0, m1, m0, m0)
            finish(part, grouped)
